import numpy as np
import ml_dtypes


def mxq(x, axis, fmt="e4m3"):
    dtype, down = {"e4m3": (ml_dtypes.float8_e4m3fn, 7), "e5m2": (ml_dtypes.float8_e5m2, 14)}[fmt]
    v = np.moveaxis(np.asarray(x, np.float32).astype(ml_dtypes.bfloat16).astype(np.float64), axis, -1)
    blocks = v.reshape(v.shape[:-1] + (-1, 32))
    amax = np.abs(blocks).max(-1, keepdims=True)
    byte = np.maximum(np.where(amax > 0, np.frexp(amax)[1] - 1 + 127, 0) - down, 1)
    scale = np.exp2(byte - 127.0)
    codes = (blocks / scale).astype(np.float32).astype(dtype).astype(np.float64)
    return np.moveaxis((codes * scale).reshape(v.shape), -1, axis)


WIDE = False


def mx_kscale(k):
    if not WIDE:
        return np.ones(k)
    levels = np.array([30, -30])
    if k % 512:
        return np.exp2(np.random.permutation(np.resize(levels, k // 32))).repeat(32)
    a = np.empty((k // 512, 16))
    for p in range(k // 512):
        a[p, :8] = np.random.permutation(np.resize(levels, 8))
        for g in range(8):
            far = levels[np.abs(levels - a[p, g]) >= 10]
            a[p, g + 8] = far[np.random.randint(len(far))]
    return np.exp2(a.ravel()).repeat(32)


def f64(x):
    return np.asarray(x).astype(np.float64)


def striped(idx):
    return np.tile(np.asarray(idx).reshape(-1, 16).T, (8, 1)).astype(np.uint16)


def unstriped(offs):
    return offs[:16].T.reshape(-1).astype(np.int64)


E2M1 = np.array([0.0, 0.5, 1.0, 1.5, 2.0, 3.0, 4.0, 6.0, -0.0, -0.5, -1.0, -1.5, -2.0, -3.0, -4.0, -6.0])


def pack_weight(w, fmt):
    k, n = w.shape
    w = f64(np.asarray(w, np.float32).astype(ml_dtypes.bfloat16)).reshape(k // 32, 32, n)
    amax = np.abs(w).max(1)
    if fmt in ("e4m3", "e5m2"):
        byte = np.frexp(amax)[1] - 1 + 127 - (7 if fmt == "e4m3" else 14)
    else:
        mant, ex = np.frexp(amax / 6.0)
        byte = np.where(mant > 0.5, ex, ex - 1) + 127
    byte = np.clip(np.where(amax > 0, byte, 1), 1, 254)
    scaled = (w * np.exp2(127.0 - byte)[:, None, :]).reshape(k, n).astype(np.float32)
    by_word = np.ascontiguousarray(scaled.reshape(k // 512, 128, 4, n).transpose(0, 1, 3, 2))
    if fmt in ("e4m3", "e5m2"):
        words = by_word.astype(ml_dtypes.float8_e4m3fn if fmt == "e4m3" else ml_dtypes.float8_e5m2).view(np.uint8)
    else:
        c = by_word.astype(ml_dtypes.float4_e2m1fn).view(np.uint8) & 0xF
        words = (c[..., 0::2] | (c[..., 1::2] << 4)).reshape(k // 512, 128, 2 * n)
    return np.ascontiguousarray(words), np.ascontiguousarray(byte.astype(np.uint8).reshape(k // 512, 16, n))


def unpack_weight(words, scales, fmt):
    g, _, n = scales.shape
    words = np.ascontiguousarray(words).reshape(g, 128, n, -1)
    if fmt in ("e4m3", "e5m2"):
        vals = words.view(ml_dtypes.float8_e4m3fn if fmt == "e4m3" else ml_dtypes.float8_e5m2).astype(np.float64)
    else:
        nib = np.empty((g, 128, n, 4), np.uint8)
        nib[..., 0::2] = words & 0xF
        nib[..., 1::2] = words >> 4
        vals = E2M1[nib]
    vals = vals * np.repeat(np.exp2(scales.astype(np.float64) - 127.0), 8, axis=1)[..., None]
    return vals.transpose(0, 1, 3, 2).reshape(g * 512, n)


K, F, T, Z, J, R, O, N, E = 512, 512, 1024, 1024, 256, 512, 256, 256, 1024


def setup_inputs():
    n = np.random.standard_normal
    idx = np.random.permutation(T)[:J]
    idx2 = np.random.permutation(Z)[:J]
    idx3 = np.random.permutation(J)[:O]
    idx4 = np.random.permutation(O)[:O]
    idx5 = np.random.permutation(T)[:O]
    idx6 = np.random.permutation(E)[:O]
    fk = mx_kscale(K)
    fr = mx_kscale(R)
    ff = mx_kscale(F)
    xtp = pack_weight(n((K, T)) / fk[:, None], "e5m2")
    wp = pack_weight(n((K, R)) * 1 / np.sqrt(K) * fk[:, None] * fr, "e2m1")
    xop = pack_weight(n((F, Z)) / ff[:, None], "e4m3")
    w0p = pack_weight(n((F, R)) * 1 / np.sqrt(F) * ff[:, None] * fr, "e2m1")
    wbp = pack_weight(n((R, N)) * 1 / np.sqrt(R) / fr[:, None], "e2m1")
    wsp = pack_weight(n((K, N)) * 1 / np.sqrt(K) * fk[:, None], "e2m1")
    return {
        "xt_words": xtp[0],
        "xt_scales": xtp[1],
        "w_words": wp[0],
        "w_scales": wp[1],
        "xo_words": xop[0],
        "xo_scales": xop[1],
        "w0_words": w0p[0],
        "w0_scales": w0p[1],
        "wb_words": wbp[0],
        "wb_scales": wbp[1],
        "ws_words": wsp[0],
        "ws_scales": wsp[1],
        "tz": (n((N, E))).astype(np.float32),
        "offs": striped(idx),
        "offs2": striped(idx2),
        "offs3": striped(idx3),
        "offs4": striped(idx4),
        "offs5": striped(idx5),
        "offs6": striped(idx6),
    }


def reference(xt_words, xt_scales, w_words, w_scales, xo_words, xo_scales, w0_words, w0_scales, wb_words, wb_scales, ws_words, ws_scales, tz, offs, offs2, offs3, offs4, offs5, offs6):
    idx = unstriped(offs)
    idx2 = unstriped(offs2)
    idx3 = unstriped(offs3)
    idx4 = unstriped(offs4)
    idx5 = unstriped(offs5)
    idx6 = unstriped(offs6)
    xtu = unpack_weight(xt_words, xt_scales, "e5m2")
    wu = unpack_weight(w_words, w_scales, "e2m1")
    xou = unpack_weight(xo_words, xo_scales, "e4m3")
    w0u = unpack_weight(w0_words, w0_scales, "e2m1")
    wbu = unpack_weight(wb_words, wb_scales, "e2m1")
    wsu = unpack_weight(ws_words, ws_scales, "e2m1")
    xtidxg = xtu[:, idx]
    xoidx2g = xou[:, idx2]
    a = wu.T @ xtidxg + w0u.T @ xoidx2g
    ca = a[:, idx3]
    hid = np.abs(ca - ca[:, idx4])
    hidq = mxq(hid, 0, "e4m3")
    xtidx5g = xtu[:, idx5]
    p = wbu.T @ hidq + wsu.T @ xtidx5g
    y = p + f64(tz)[:, idx6]
    return y

@@ -1,0 +1,207 @@
+from contextlib import ExitStack
+
+import concourse.mybir as mybir
+
+K, F, T, Z, J, R, O, N, E = 512, 512, 1024, 1024, 256, 512, 256, 256, 1024
+FLOPS = 2 * (K * R * J + F * R * J + R * N * O + K * N * O)
+
+F32 = mybir.dt.float32
+BF16 = mybir.dt.bfloat16
+I32 = mybir.dt.int32
+U32 = mybir.dt.uint32
+U16 = mybir.dt.uint16
+U8 = mybir.dt.uint8
+E4M3 = mybir.dt.float8_e4m3fn_x4
+E5M2 = mybir.dt.float8_e5m2_x4
+E2M1 = mybir.dt.float4_e2m1fn_x4
+ACT = mybir.ActivationFunctionType
+ALU = mybir.AluOpType
+
+P = 128
+PACK = 4
+HALF = O // 2
+A_COLS = 352
+
+
+def tile_list_neighbours_bank_further_tabled_kernel(
+    tc, xt_words, xt_scales, w_words, w_scales, xo_words, xo_scales, w0_words, w0_scales,
+    wb_words, wb_scales, ws_words, ws_scales, tz, offs, offs2, offs3, offs4, offs5, offs6, out,
+):
+    nc = tc.nc
+    with ExitStack() as ctx:
+        keep = ctx.enter_context(tc.tile_pool(name="keep", bufs=1))
+        psum = ctx.enter_context(tc.psum_pool(name="psum", bufs=1))
+
+        def sb(name, shape, dtype):
+            return keep.tile(shape, dtype, name=name, align_bytes=64)
+
+        l1, l2, l3, l4, l5, l6 = [sb("list%d" % i, [P, 16], U16) for i in range(1, 7)]
+        xt_w = sb("xt_w", [P, T], I32)
+        xo_w = sb("xo_w", [P, Z], I32)
+        xt_s = sb("xt_s", [P, T], U8)
+        xo_s = sb("xo_s", [P, Z], U8)
+        w_raw = sb("w_raw", [P, 2 * R], U8)
+        w0_raw = sb("w0_raw", [P, 2 * R], U8)
+        s1 = sb("s1", [P, 2 * R], U8)
+        w_sraw, w0_sraw = s1[:, :R], s1[:, R:]
+        ws_s, wb_s, g5_s = s1[:, :N], s1[:, N : 2 * N], s1[:, 2 * N : 3 * N]
+        sa = sb("sa", [P, J + R], U8)
+        sc = sb("sc", [P, J + R], U8)
+        gx_s, w_sd = sa[:, :J], sa[:, J:]
+        go_s, w0_sd = sc[:, :J], sc[:, J:]
+        a = [sb("a%d" % t, [P, A_COLS], F32) for t in range(PACK)]
+
+        def spread_scales(dst, src):
+            for q in range(1, 4):
+                nc.sync.dma_start(dst[32 * q : 32 * q + 4, :].bitcast(I32), src[4 * q : 4 * q + 4, :].bitcast(I32))
+
+        nc.vector.memset(xt_s[:].bitcast(I32), 0)
+        nc.vector.memset(s1[:].bitcast(I32), 0)
+        nc.vector.memset(xo_s[:].bitcast(I32), 0)
+
+        nc.sync.dma_start(l1[:], offs)
+        nc.scalar.dma_start(xt_w[:], xt_words[0].rearrange("p c r -> p (c r)").bitcast(I32))
+        nc.sync.dma_start(xt_s[:16, :].bitcast(I32), xt_scales[0].bitcast(I32))
+        nc.scalar.dma_start(xo_w[:], xo_words[0].rearrange("p c r -> p (c r)").bitcast(I32))
+        nc.sync.dma_start(s1[:16, :R].bitcast(I32), w_scales[0].bitcast(I32))
+        nc.sync.dma_start(l2[:], offs2)
+        nc.sync.dma_start(xo_s[:16, :].bitcast(I32), xo_scales[0].bitcast(I32))
+        nc.sync.dma_start(s1[:16, R:].bitcast(I32), w0_scales[0].bitcast(I32))
+        nc.sync.dma_start(w_raw[:].bitcast(I32), w_words[0].bitcast(I32))
+        nc.sync.dma_start(w0_raw[:].bitcast(I32), w0_words[0].bitcast(I32))
+        nc.sync.dma_start(l5[:], offs5)
+        for t in range(PACK):
+            nc.vector.memset(a[t][:, J:], 0.0)
+
+        def gather_words(name, table, lst):
+            g = sb(name, [P, J], U32)
+            nc.vector.tensor_copy(g[:], table[:].bitcast(U32).indirect(lst[:]))
+            return g
+
+        def deal_words(name, raw):
+            d = sb(name, [P, 2 * R], U8)
+            nc.scalar.copy(
+                d[:].bitcast(U16).rearrange("p (t m) -> p t m", t=PACK),
+                raw[:].bitcast(U16).rearrange("p (m t) -> p t m", t=PACK),
+            )
+            return d
+
+        def deal_bytes(dst, raw):
+            nc.vector.tensor_copy(dst.rearrange("p (t m) -> p t m", t=PACK), raw.rearrange("p (m t) -> p t m", t=PACK))
+
+        def stage_scales(name, plane, table, lst, raw):
+            g = sb(name, [P, J], U8)
+            nc.vector.tensor_copy(g[:], table[:].indirect(lst[:]))
+            deal_bytes(plane[:, J:], raw)
+            nc.vector.tensor_copy(plane[:, :J].bitcast(I32), g[:].bitcast(I32))
+            spread_scales(plane[:], plane[:])
+
+        stage_scales("gx_raw", sa, xt_s, l1, w_sraw)
+        stage_scales("go_raw", sc, xo_s, l2, w0_sraw)
+        nc.sync.dma_start(l3[:], offs3)
+        nc.sync.dma_start(l4[:], offs4)
+        nc.sync.dma_start(l6[:], offs6)
+        gx_w = gather_words("gx_w", xt_w, l1)
+        w_d = deal_words("w_d", w_raw)
+        w0_d = deal_words("w0_d", w0_raw)
+        go_w = gather_words("go_w", xo_w, l2)
+        g5_w = gather_words("g5_w", xt_w, l5)
+        g5_raw = sb("g5_raw", [P, O], U8)
+        nc.vector.tensor_copy(g5_raw[:], xt_s[:].indirect(l5[:]))
+
+        w2 = keep.tile([P, 4 * N], U8, name="w2", tag="w_raw", align_bytes=64)
+        ws_w, wb_w = w2[:, : 2 * N], w2[:, 2 * N :]
+        nc.sync.dma_start(ws_w.bitcast(I32), ws_words[0].bitcast(I32))
+        nc.sync.dma_start(wb_w.bitcast(I32), wb_words[0].bitcast(I32))
+        nc.sync.dma_start(ws_s[:16, :].bitcast(I32), ws_scales[0].bitcast(I32))
+        nc.sync.dma_start(wb_s[:16, :].bitcast(I32), wb_scales[0].bitcast(I32))
+        nc.vector.tensor_copy(g5_s.bitcast(I32), g5_raw[:].bitcast(I32))
+        spread_scales(s1[:, : 3 * N], s1[:, : 3 * N])
+
+        tz_sb = [keep.tile([P, E], F32, name="tz%d" % n, tag=tag, align_bytes=64) for n, tag in enumerate(("xo_w", "xt_w"))]
+        for n in range(2):
+            nc.sync.dma_start(tz_sb[n][:], tz[P * n : P * (n + 1), :])
+
+        pa = [psum.tile([P, J], F32, name="pa%d" % t) for t in range(PACK)]
+        for t in range(PACK):
+            nc.tensor.matmul_mx(
+                pa[t][:], lhsT=w_d[:, 2 * P * t : 2 * P * (t + 1)].bitcast(E2M1), lhsT_scale=w_sd[:, P * t : P * (t + 1)],
+                rhs=gx_w[:].bitcast(E5M2), rhs_scale=gx_s, start=True, stop=False,
+            )
+        for t in range(PACK):
+            nc.tensor.matmul_mx(
+                pa[t][:], lhsT=w0_d[:, 2 * P * t : 2 * P * (t + 1)].bitcast(E2M1), lhsT_scale=w0_sd[:, P * t : P * (t + 1)],
+                rhs=go_w[:].bitcast(E4M3), rhs_scale=go_s, start=False, stop=True,
+            )
+
+        po = [psum.tile([P, 2, HALF], F32, name="po%d" % h) for h in range(2)]
+        for h in range(2):
+            cols = slice(HALF * h, HALF * (h + 1))
+            for n in range(2):
+                nc.tensor.matmul_mx(
+                    po[h][:, n, :], lhsT=ws_w[:, 2 * P * n : 2 * P * (n + 1)].bitcast(E2M1), lhsT_scale=ws_s[:, P * n : P * (n + 1)],
+                    rhs=g5_w[:, cols].bitcast(E5M2), rhs_scale=g5_s[:, cols], start=(n == 0), stop=False,
+                )
+
+        def gather_f32(on_vector, dst, window, lst):
+            if on_vector:
+                nc.vector.tensor_copy(dst, window.indirect(lst))
+            else:
+                nc.scalar.activation(dst, window.indirect(lst), ACT.Copy)
+
+        ca = [sb("ca%d" % t, [P, O], F32) for t in range(PACK)]
+        diff = [sb("diff%d" % h, [P, PACK, HALF], F32) for h in range(2)]
+        cb = {}
+
+        def leave_bank(t):
+            if t % 2 == 0:
+                nc.vector.tensor_copy(a[t][:, :J], pa[t][:])
+            else:
+                nc.scalar.activation(a[t][:, :J], pa[t][:], ACT.Copy)
+
+        def take_slots(t):
+            gather_f32(t % 2 == 0, ca[t][:], a[t][:], l3[:])
+
+        def take_neighbours(t, h):
+            tag = "a%d" % (t + 2) if (t < 2 and h == 1) else "cb%d%d" % (t, h)
+            cb[t, h] = keep.tile([P, HALF], F32, name="cb%d%d" % (t, h), tag=tag, align_bytes=64)
+            gather_f32(t % 2 == 0, cb[t, h][:], ca[t][:], l4[:, 8 * h : 8 * (h + 1)])
+
+        def subtract(t, h):
+            nc.vector.tensor_tensor(diff[h][:, t, :], ca[t][:, HALF * h : HALF * (h + 1)], cb[t, h][:], ALU.subtract)
+
+        for t in (0, 1):
+            leave_bank(t)
+            take_slots(t)
+        for t in (0, 1):
+            leave_bank(t + 2)
+            take_neighbours(t, 0)
+            take_slots(t + 2)
+            take_neighbours(t, 1)
+        for h in range(2):
+            for t in (2, 3):
+                take_neighbours(t, h)
+            for t in range(PACK):
+                subtract(t, h)
+
+        for h in range(2):
+            hid = sb("hid%d" % h, [P, HALF, PACK], BF16)
+            nc.scalar.activation(
+                hid[:].rearrange("p (c i) t -> p c t i", i=4), diff[h][:].rearrange("p t (c i) -> p c t i", i=4), ACT.Abs
+            )
+            hq_w = sb("hq_w%d" % h, [P, HALF], U32)
+            hq_s = sb("hq_s%d" % h, [P, HALF], U8)
+            nc.vector.quantize_mx(hq_w[:].bitcast(E4M3), hq_s[:], hid[:].rearrange("p c t -> p (c t)"))
+            for n in range(2):
+                nc.tensor.matmul_mx(
+                    po[h][:, n, :], lhsT=wb_w[:, 2 * P * n : 2 * P * (n + 1)].bitcast(E2M1), lhsT_scale=wb_s[:, P * n : P * (n + 1)],
+                    rhs=hq_w[:].bitcast(E4M3), rhs_scale=hq_s[:], start=False, stop=(n == 1),
+                )
+        tzg = keep.tile([P, 2, 2, HALF], F32, name="tzg", tag="diff1", align_bytes=64)
+        for h in range(2):
+            cols = slice(HALF * h, HALF * (h + 1))
+            for n in range(2):
+                gather_f32(False, tzg[:, h, n, :], tz_sb[n][:], l6[:, 8 * h : 8 * (h + 1)])
+            res = sb("res%d" % h, [P, 2, HALF], F32)
+            nc.vector.tensor_tensor(res[:], po[h][:], tzg[:, h, :, :], ALU.add)
+            nc.sync.dma_start(out.rearrange("(n p) o -> p n o", p=P)[:, :, cols], res[:])

@@ -51,23 +51,23 @@ def tile_list_neighbours_bank_further_tabled_kernel(
         go_s, w0_sd = sc[:, :J], sc[:, J:]
         a = [sb("a%d" % t, [P, A_COLS], F32) for t in range(PACK)]
 
-        def spread_scales(dst, src):
-            for q in range(1, 4):
-                nc.sync.dma_start(dst[32 * q : 32 * q + 4, :].bitcast(I32), src[4 * q : 4 * q + 4, :].bitcast(I32))
+        def spread_scales(dst, src, queues=(nc.sync, nc.sync, nc.sync)):
+            for q, queue in zip(range(1, 4), queues):
+                queue.dma_start(dst[32 * q : 32 * q + 4, :].bitcast(I32), src[4 * q : 4 * q + 4, :].bitcast(I32))
 
         nc.vector.memset(xt_s[:].bitcast(I32), 0)
         nc.vector.memset(s1[:].bitcast(I32), 0)
         nc.vector.memset(xo_s[:].bitcast(I32), 0)
 
         nc.sync.dma_start(l1[:], offs)
-        nc.scalar.dma_start(xt_w[:], xt_words[0].rearrange("p c r -> p (c r)").bitcast(I32))
+        nc.scalar.dma_start(w_raw[:].bitcast(I32), w_words[0].bitcast(I32))
         nc.sync.dma_start(xt_s[:16, :].bitcast(I32), xt_scales[0].bitcast(I32))
-        nc.scalar.dma_start(xo_w[:], xo_words[0].rearrange("p c r -> p (c r)").bitcast(I32))
-        nc.sync.dma_start(s1[:16, :R].bitcast(I32), w_scales[0].bitcast(I32))
+        nc.scalar.dma_start(s1[:16, :R].bitcast(I32), w_scales[0].bitcast(I32))
+        nc.scalar.dma_start(s1[:16, R:].bitcast(I32), w0_scales[0].bitcast(I32))
         nc.sync.dma_start(l2[:], offs2)
         nc.sync.dma_start(xo_s[:16, :].bitcast(I32), xo_scales[0].bitcast(I32))
-        nc.sync.dma_start(s1[:16, R:].bitcast(I32), w0_scales[0].bitcast(I32))
-        nc.sync.dma_start(w_raw[:].bitcast(I32), w_words[0].bitcast(I32))
+        nc.sync.dma_start(xt_w[:], xt_words[0].rearrange("p c r -> p (c r)").bitcast(I32))
+        nc.sync.dma_start(xo_w[:], xo_words[0].rearrange("p c r -> p (c r)").bitcast(I32))
         nc.sync.dma_start(w0_raw[:].bitcast(I32), w0_words[0].bitcast(I32))
         nc.sync.dma_start(l5[:], offs5)
         for t in range(PACK):
@@ -94,13 +94,17 @@ def tile_list_neighbours_bank_further_tabled_kernel(
             nc.vector.tensor_copy(g[:], table[:].indirect(lst[:]))
             deal_bytes(plane[:, J:], raw)
             nc.vector.tensor_copy(plane[:, :J].bitcast(I32), g[:].bitcast(I32))
-            spread_scales(plane[:], plane[:])
+            spread_scales(plane[:], plane[:], (nc.sync, nc.scalar, nc.sync))
 
         stage_scales("gx_raw", sa, xt_s, l1, w_sraw)
         stage_scales("go_raw", sc, xo_s, l2, w0_sraw)
+        tz_sb = [sb("tz%d" % n, [P, E], F32) for n in range(2)]
+        nc.sync.dma_start(tz_sb[0][:], tz[:P, :])
         nc.sync.dma_start(l3[:], offs3)
         nc.sync.dma_start(l4[:], offs4)
         nc.sync.dma_start(l6[:], offs6)
+        nc.sync.dma_start(ws_s[:16, :].bitcast(I32), ws_scales[0].bitcast(I32))
+        nc.sync.dma_start(wb_s[:16, :].bitcast(I32), wb_scales[0].bitcast(I32))
         gx_w = gather_words("gx_w", xt_w, l1)
         w_d = deal_words("w_d", w_raw)
         w0_d = deal_words("w0_d", w0_raw)
@@ -109,18 +113,13 @@ def tile_list_neighbours_bank_further_tabled_kernel(
         g5_raw = sb("g5_raw", [P, O], U8)
         nc.vector.tensor_copy(g5_raw[:], xt_s[:].indirect(l5[:]))
 
-        w2 = keep.tile([P, 4 * N], U8, name="w2", tag="w_raw", align_bytes=64)
+        w2 = keep.tile([P, 4 * N], U8, name="w2", tag="w0_raw", align_bytes=64)
         ws_w, wb_w = w2[:, : 2 * N], w2[:, 2 * N :]
         nc.sync.dma_start(ws_w.bitcast(I32), ws_words[0].bitcast(I32))
-        nc.sync.dma_start(wb_w.bitcast(I32), wb_words[0].bitcast(I32))
-        nc.sync.dma_start(ws_s[:16, :].bitcast(I32), ws_scales[0].bitcast(I32))
-        nc.sync.dma_start(wb_s[:16, :].bitcast(I32), wb_scales[0].bitcast(I32))
         nc.vector.tensor_copy(g5_s.bitcast(I32), g5_raw[:].bitcast(I32))
         spread_scales(s1[:, : 3 * N], s1[:, : 3 * N])
-
-        tz_sb = [keep.tile([P, E], F32, name="tz%d" % n, tag=tag, align_bytes=64) for n, tag in enumerate(("xo_w", "xt_w"))]
-        for n in range(2):
-            nc.sync.dma_start(tz_sb[n][:], tz[P * n : P * (n + 1), :])
+        nc.sync.dma_start(wb_w.bitcast(I32), wb_words[0].bitcast(I32))
+        nc.sync.dma_start(tz_sb[1][:], tz[P:, :])
 
         pa = [psum.tile([P, J], F32, name="pa%d" % t) for t in range(PACK)]
         for t in range(PACK):
@@ -134,13 +133,13 @@ def tile_list_neighbours_bank_further_tabled_kernel(
                 rhs=go_w[:].bitcast(E4M3), rhs_scale=go_s, start=False, stop=True,
             )
 
-        po = [psum.tile([P, 2, HALF], F32, name="po%d" % h) for h in range(2)]
+        po = {(h, n): psum.tile([P, HALF], F32, name="po%d%d" % (h, n)) for h in range(2) for n in range(2)}
         for h in range(2):
             cols = slice(HALF * h, HALF * (h + 1))
             for n in range(2):
                 nc.tensor.matmul_mx(
-                    po[h][:, n, :], lhsT=ws_w[:, 2 * P * n : 2 * P * (n + 1)].bitcast(E2M1), lhsT_scale=ws_s[:, P * n : P * (n + 1)],
-                    rhs=g5_w[:, cols].bitcast(E5M2), rhs_scale=g5_s[:, cols], start=(n == 0), stop=False,
+                    po[h, n][:], lhsT=ws_w[:, 2 * P * n : 2 * P * (n + 1)].bitcast(E2M1), lhsT_scale=ws_s[:, P * n : P * (n + 1)],
+                    rhs=g5_w[:, cols].bitcast(E5M2), rhs_scale=g5_s[:, cols], start=True, stop=False,
                 )
 
         def gather_f32(on_vector, dst, window, lst):
@@ -149,59 +148,60 @@ def tile_list_neighbours_bank_further_tabled_kernel(
             else:
                 nc.scalar.activation(dst, window.indirect(lst), ACT.Copy)
 
-        ca = [sb("ca%d" % t, [P, O], F32) for t in range(PACK)]
+        owner = {0: (0, 0), 3: (0, 1), 1: (1, 0), 2: (1, 1)}
+        ca = [sb("ca%d" % e, [P, 2, O], F32) for e in range(2)]
         diff = [sb("diff%d" % h, [P, PACK, HALF], F32) for h in range(2)]
-        cb = {}
+        cb = {(e, h): sb("cb%d%d" % (e, h), [P, 2, HALF], F32) for e in range(2) for h in range(2)}
 
-        def leave_bank(t):
-            if t % 2 == 0:
+        for t in range(PACK):
+            e, i = owner[t]
+            if e == 0:
                 nc.vector.tensor_copy(a[t][:, :J], pa[t][:])
             else:
                 nc.scalar.activation(a[t][:, :J], pa[t][:], ACT.Copy)
-
-        def take_slots(t):
-            gather_f32(t % 2 == 0, ca[t][:], a[t][:], l3[:])
-
-        def take_neighbours(t, h):
-            tag = "a%d" % (t + 2) if (t < 2 and h == 1) else "cb%d%d" % (t, h)
-            cb[t, h] = keep.tile([P, HALF], F32, name="cb%d%d" % (t, h), tag=tag, align_bytes=64)
-            gather_f32(t % 2 == 0, cb[t, h][:], ca[t][:], l4[:, 8 * h : 8 * (h + 1)])
-
-        def subtract(t, h):
-            nc.vector.tensor_tensor(diff[h][:, t, :], ca[t][:, HALF * h : HALF * (h + 1)], cb[t, h][:], ALU.subtract)
-
-        for t in (0, 1):
-            leave_bank(t)
-            take_slots(t)
-        for t in (0, 1):
-            leave_bank(t + 2)
-            take_neighbours(t, 0)
-            take_slots(t + 2)
-            take_neighbours(t, 1)
+        for t in range(PACK):
+            e, i = owner[t]
+            gather_f32(e == 0, ca[e][:, i, :], a[t][:], l3[:])
         for h in range(2):
-            for t in (2, 3):
-                take_neighbours(t, h)
             for t in range(PACK):
-                subtract(t, h)
+                e, i = owner[t]
+                gather_f32(e == 0, cb[e, h][:, i, :], ca[e][:, i, :], l4[:, 8 * h : 8 * (h + 1)])
+            for t in (0, 1, 3, 2):
+                e, i = owner[t]
+                nc.vector.tensor_tensor(
+                    diff[h][:, t, :], ca[e][:, i, HALF * h : HALF * (h + 1)], cb[e, h][:, i, :], ALU.subtract
+                )
 
+        first = keep.tile([P, HALF], F32, name="tzg_first", tag="a2", align_bytes=64)
+        others = keep.tile([P, 3, HALF], F32, name="tzg_others", tag="diff1", align_bytes=64)
+        tzg = {(0, 0): first[:], (0, 1): others[:, 0, :], (1, 0): others[:, 1, :], (1, 1): others[:, 2, :]}
         for h in range(2):
             hid = sb("hid%d" % h, [P, HALF, PACK], BF16)
+            cut = (HALF, HALF // 2)[h]
             nc.scalar.activation(
-                hid[:].rearrange("p (c i) t -> p c t i", i=4), diff[h][:].rearrange("p t (c i) -> p c t i", i=4), ACT.Abs
+                hid[:, :cut, :].rearrange("p (c i) t -> p c t i", i=4),
+                diff[h][:, :, :cut].rearrange("p t (c i) -> p c t i", i=4),
+                ACT.Abs,
             )
+            if h == 1:
+                rest = diff[h][:, :, cut:].rearrange("p t c -> p c t")
+                nc.vector.scalar_tensor_tensor(hid[:, cut:, :], rest, -1.0, rest, ALU.mult, ALU.max)
             hq_w = sb("hq_w%d" % h, [P, HALF], U32)
             hq_s = sb("hq_s%d" % h, [P, HALF], U8)
             nc.vector.quantize_mx(hq_w[:].bitcast(E4M3), hq_s[:], hid[:].rearrange("p c t -> p (c t)"))
             for n in range(2):
                 nc.tensor.matmul_mx(
-                    po[h][:, n, :], lhsT=wb_w[:, 2 * P * n : 2 * P * (n + 1)].bitcast(E2M1), lhsT_scale=wb_s[:, P * n : P * (n + 1)],
-                    rhs=hq_w[:].bitcast(E4M3), rhs_scale=hq_s[:], start=False, stop=(n == 1),
+                    po[h, n][:], lhsT=wb_w[:, 2 * P * n : 2 * P * (n + 1)].bitcast(E2M1), lhsT_scale=wb_s[:, P * n : P * (n + 1)],
+                    rhs=hq_w[:].bitcast(E4M3), rhs_scale=hq_s[:], start=False, stop=True,
                 )
-        tzg = keep.tile([P, 2, 2, HALF], F32, name="tzg", tag="diff1", align_bytes=64)
         for h in range(2):
             cols = slice(HALF * h, HALF * (h + 1))
             for n in range(2):
-                gather_f32(False, tzg[:, h, n, :], tz_sb[n][:], l6[:, 8 * h : 8 * (h + 1)])
+                gather_f32(False, tzg[h, n], tz_sb[n][:], l6[:, 8 * h : 8 * (h + 1)])
             res = sb("res%d" % h, [P, 2, HALF], F32)
-            nc.vector.tensor_tensor(res[:], po[h][:], tzg[:, h, :, :], ALU.add)
-            nc.sync.dma_start(out.rearrange("(n p) o -> p n o", p=P)[:, :, cols], res[:])
+            for n in range(2):
+                nc.vector.tensor_tensor(res[:, n, :], po[h, n][:], tzg[h, n], ALU.add)
+                if h == 1:
+                    (nc.sync, nc.scalar)[n].dma_start(out[P * n : P * (n + 1), cols], res[:, n, :])
+            if h == 0:
+                nc.sync.dma_start(out.rearrange("(n p) o -> p n o", p=P)[:, :, cols], res[:])

@@ -94,17 +94,13 @@ def tile_list_neighbours_bank_further_tabled_kernel(
             nc.vector.tensor_copy(g[:], table[:].indirect(lst[:]))
             deal_bytes(plane[:, J:], raw)
             nc.vector.tensor_copy(plane[:, :J].bitcast(I32), g[:].bitcast(I32))
-            spread_scales(plane[:], plane[:], (nc.sync, nc.scalar, nc.sync))
+            spread_scales(plane[:], plane[:])
 
         stage_scales("gx_raw", sa, xt_s, l1, w_sraw)
         stage_scales("go_raw", sc, xo_s, l2, w0_sraw)
-        tz_sb = [sb("tz%d" % n, [P, E], F32) for n in range(2)]
-        nc.sync.dma_start(tz_sb[0][:], tz[:P, :])
         nc.sync.dma_start(l3[:], offs3)
         nc.sync.dma_start(l4[:], offs4)
         nc.sync.dma_start(l6[:], offs6)
-        nc.sync.dma_start(ws_s[:16, :].bitcast(I32), ws_scales[0].bitcast(I32))
-        nc.sync.dma_start(wb_s[:16, :].bitcast(I32), wb_scales[0].bitcast(I32))
         gx_w = gather_words("gx_w", xt_w, l1)
         w_d = deal_words("w_d", w_raw)
         w0_d = deal_words("w0_d", w0_raw)
@@ -116,10 +112,15 @@ def tile_list_neighbours_bank_further_tabled_kernel(
         w2 = keep.tile([P, 4 * N], U8, name="w2", tag="w0_raw", align_bytes=64)
         ws_w, wb_w = w2[:, : 2 * N], w2[:, 2 * N :]
         nc.sync.dma_start(ws_w.bitcast(I32), ws_words[0].bitcast(I32))
+        nc.sync.dma_start(wb_w.bitcast(I32), wb_words[0].bitcast(I32))
+        nc.sync.dma_start(ws_s[:16, :].bitcast(I32), ws_scales[0].bitcast(I32))
+        nc.sync.dma_start(wb_s[:16, :].bitcast(I32), wb_scales[0].bitcast(I32))
         nc.vector.tensor_copy(g5_s.bitcast(I32), g5_raw[:].bitcast(I32))
         spread_scales(s1[:, : 3 * N], s1[:, : 3 * N])
-        nc.sync.dma_start(wb_w.bitcast(I32), wb_words[0].bitcast(I32))
-        nc.sync.dma_start(tz_sb[1][:], tz[P:, :])
+
+        tz_sb = [keep.tile([P, E], F32, name="tz%d" % n, tag=tag, align_bytes=64) for n, tag in enumerate(("xo_w", "xt_w"))]
+        for n in range(2):
+            nc.sync.dma_start(tz_sb[n][:], tz[P * n : P * (n + 1), :])
 
         pa = [psum.tile([P, J], F32, name="pa%d" % t) for t in range(PACK)]
         for t in range(PACK):

from contextlib import ExitStack

import concourse.mybir as mybir

K, F, T, Z, J, R, O, N, E = 512, 512, 1024, 1024, 256, 512, 256, 256, 1024
FLOPS = 2 * (K * R * J + F * R * J + R * N * O + K * N * O)

F32 = mybir.dt.float32
BF16 = mybir.dt.bfloat16
I32 = mybir.dt.int32
U32 = mybir.dt.uint32
U16 = mybir.dt.uint16
U8 = mybir.dt.uint8
E4M3 = mybir.dt.float8_e4m3fn_x4
E5M2 = mybir.dt.float8_e5m2_x4
E2M1 = mybir.dt.float4_e2m1fn_x4
ACT = mybir.ActivationFunctionType
ALU = mybir.AluOpType

P = 128
PACK = 4
HALF = O // 2
A_COLS = 352


def tile_list_neighbours_bank_further_tabled_kernel(
    tc, xt_words, xt_scales, w_words, w_scales, xo_words, xo_scales, w0_words, w0_scales,
    wb_words, wb_scales, ws_words, ws_scales, tz, offs, offs2, offs3, offs4, offs5, offs6, out,
):
    nc = tc.nc
    with ExitStack() as ctx:
        keep = ctx.enter_context(tc.tile_pool(name="keep", bufs=1))
        psum = ctx.enter_context(tc.psum_pool(name="psum", bufs=1))

        def sb(name, shape, dtype):
            return keep.tile(shape, dtype, name=name, align_bytes=64)

        l1, l2, l3, l4, l5, l6 = [sb("list%d" % i, [P, 16], U16) for i in range(1, 7)]
        xt_w = sb("xt_w", [P, T], I32)
        xo_w = sb("xo_w", [P, Z], I32)
        xt_s = sb("xt_s", [P, T], U8)
        xo_s = sb("xo_s", [P, Z], U8)
        w_raw = sb("w_raw", [P, 2 * R], U8)
        w0_raw = sb("w0_raw", [P, 2 * R], U8)
        s1 = sb("s1", [P, 2 * R], U8)
        w_sraw, w0_sraw = s1[:, :R], s1[:, R:]
        ws_s, wb_s, g5_s = s1[:, :N], s1[:, N : 2 * N], s1[:, 2 * N : 3 * N]
        sa = sb("sa", [P, J + R], U8)
        sc = sb("sc", [P, J + R], U8)
        gx_s, w_sd = sa[:, :J], sa[:, J:]
        go_s, w0_sd = sc[:, :J], sc[:, J:]
        a = [sb("a%d" % t, [P, A_COLS], F32) for t in range(PACK)]

        def spread_scales(dst, src, queues=(nc.sync, nc.sync, nc.sync)):
            for q, queue in zip(range(1, 4), queues):
                queue.dma_start(dst[32 * q : 32 * q + 4, :].bitcast(I32), src[4 * q : 4 * q + 4, :].bitcast(I32))

        nc.vector.memset(xt_s[:].bitcast(I32), 0)
        nc.vector.memset(s1[:].bitcast(I32), 0)
        nc.vector.memset(xo_s[:].bitcast(I32), 0)

        nc.sync.dma_start(l1[:], offs)
        nc.scalar.dma_start(w_raw[:].bitcast(I32), w_words[0].bitcast(I32))
        nc.sync.dma_start(xt_s[:16, :].bitcast(I32), xt_scales[0].bitcast(I32))
        nc.scalar.dma_start(s1[:16, :R].bitcast(I32), w_scales[0].bitcast(I32))
        nc.scalar.dma_start(s1[:16, R:].bitcast(I32), w0_scales[0].bitcast(I32))
        nc.sync.dma_start(l2[:], offs2)
        nc.sync.dma_start(xo_s[:16, :].bitcast(I32), xo_scales[0].bitcast(I32))
        nc.sync.dma_start(xt_w[:], xt_words[0].rearrange("p c r -> p (c r)").bitcast(I32))
        nc.sync.dma_start(xo_w[:], xo_words[0].rearrange("p c r -> p (c r)").bitcast(I32))
        nc.sync.dma_start(w0_raw[:].bitcast(I32), w0_words[0].bitcast(I32))
        nc.sync.dma_start(l5[:], offs5)
        for t in range(PACK):
            nc.vector.memset(a[t][:, J:], 0.0)

        def gather_words(name, table, lst):
            g = sb(name, [P, J], U32)
            nc.vector.tensor_copy(g[:], table[:].bitcast(U32).indirect(lst[:]))
            return g

        def deal_words(name, raw):
            d = sb(name, [P, 2 * R], U8)
            nc.scalar.copy(
                d[:].bitcast(U16).rearrange("p (t m) -> p t m", t=PACK),
                raw[:].bitcast(U16).rearrange("p (m t) -> p t m", t=PACK),
            )
            return d

        def deal_bytes(dst, raw):
            nc.vector.tensor_copy(dst.rearrange("p (t m) -> p t m", t=PACK), raw.rearrange("p (m t) -> p t m", t=PACK))

        def stage_scales(name, plane, table, lst, raw):
            g = sb(name, [P, J], U8)
            nc.vector.tensor_copy(g[:], table[:].indirect(lst[:]))
            deal_bytes(plane[:, J:], raw)
            nc.vector.tensor_copy(plane[:, :J].bitcast(I32), g[:].bitcast(I32))
            spread_scales(plane[:], plane[:])

        stage_scales("gx_raw", sa, xt_s, l1, w_sraw)
        stage_scales("go_raw", sc, xo_s, l2, w0_sraw)
        nc.sync.dma_start(l3[:], offs3)
        nc.sync.dma_start(l4[:], offs4)
        nc.sync.dma_start(l6[:], offs6)
        gx_w = gather_words("gx_w", xt_w, l1)
        w_d = deal_words("w_d", w_raw)
        w0_d = deal_words("w0_d", w0_raw)
        go_w = gather_words("go_w", xo_w, l2)
        g5_w = gather_words("g5_w", xt_w, l5)
        g5_raw = sb("g5_raw", [P, O], U8)
        nc.vector.tensor_copy(g5_raw[:], xt_s[:].indirect(l5[:]))

        w2 = keep.tile([P, 4 * N], U8, name="w2", tag="w0_raw", align_bytes=64)
        ws_w, wb_w = w2[:, : 2 * N], w2[:, 2 * N :]
        nc.sync.dma_start(ws_w.bitcast(I32), ws_words[0].bitcast(I32))
        nc.sync.dma_start(wb_w.bitcast(I32), wb_words[0].bitcast(I32))
        nc.sync.dma_start(ws_s[:16, :].bitcast(I32), ws_scales[0].bitcast(I32))
        nc.sync.dma_start(wb_s[:16, :].bitcast(I32), wb_scales[0].bitcast(I32))
        nc.vector.tensor_copy(g5_s.bitcast(I32), g5_raw[:].bitcast(I32))
        spread_scales(s1[:, : 3 * N], s1[:, : 3 * N])

        tz_sb = [keep.tile([P, E], F32, name="tz%d" % n, tag=tag, align_bytes=64) for n, tag in enumerate(("xo_w", "xt_w"))]
        for n in range(2):
            nc.sync.dma_start(tz_sb[n][:], tz[P * n : P * (n + 1), :])

        pa = [psum.tile([P, J], F32, name="pa%d" % t) for t in range(PACK)]
        for t in range(PACK):
            nc.tensor.matmul_mx(
                pa[t][:], lhsT=w_d[:, 2 * P * t : 2 * P * (t + 1)].bitcast(E2M1), lhsT_scale=w_sd[:, P * t : P * (t + 1)],
                rhs=gx_w[:].bitcast(E5M2), rhs_scale=gx_s, start=True, stop=False,
            )
        for t in range(PACK):
            nc.tensor.matmul_mx(
                pa[t][:], lhsT=w0_d[:, 2 * P * t : 2 * P * (t + 1)].bitcast(E2M1), lhsT_scale=w0_sd[:, P * t : P * (t + 1)],
                rhs=go_w[:].bitcast(E4M3), rhs_scale=go_s, start=False, stop=True,
            )

        po = {(h, n): psum.tile([P, HALF], F32, name="po%d%d" % (h, n)) for h in range(2) for n in range(2)}
        for h in range(2):
            cols = slice(HALF * h, HALF * (h + 1))
            for n in range(2):
                nc.tensor.matmul_mx(
                    po[h, n][:], lhsT=ws_w[:, 2 * P * n : 2 * P * (n + 1)].bitcast(E2M1), lhsT_scale=ws_s[:, P * n : P * (n + 1)],
                    rhs=g5_w[:, cols].bitcast(E5M2), rhs_scale=g5_s[:, cols], start=True, stop=False,
                )

        def gather_f32(on_vector, dst, window, lst):
            if on_vector:
                nc.vector.tensor_copy(dst, window.indirect(lst))
            else:
                nc.scalar.activation(dst, window.indirect(lst), ACT.Copy)

        owner = {0: (0, 0), 3: (0, 1), 1: (1, 0), 2: (1, 1)}
        ca = [sb("ca%d" % e, [P, 2, O], F32) for e in range(2)]
        diff = [sb("diff%d" % h, [P, PACK, HALF], F32) for h in range(2)]
        cb = {(e, h): sb("cb%d%d" % (e, h), [P, 2, HALF], F32) for e in range(2) for h in range(2)}

        for t in range(PACK):
            e, i = owner[t]
            if e == 0:
                nc.vector.tensor_copy(a[t][:, :J], pa[t][:])
            else:
                nc.scalar.activation(a[t][:, :J], pa[t][:], ACT.Copy)
        for t in range(PACK):
            e, i = owner[t]
            gather_f32(e == 0, ca[e][:, i, :], a[t][:], l3[:])
        for h in range(2):
            for t in range(PACK):
                e, i = owner[t]
                gather_f32(e == 0, cb[e, h][:, i, :], ca[e][:, i, :], l4[:, 8 * h : 8 * (h + 1)])
            for t in (0, 1, 3, 2):
                e, i = owner[t]
                nc.vector.tensor_tensor(
                    diff[h][:, t, :], ca[e][:, i, HALF * h : HALF * (h + 1)], cb[e, h][:, i, :], ALU.subtract
                )

        first = keep.tile([P, HALF], F32, name="tzg_first", tag="a2", align_bytes=64)
        others = keep.tile([P, 3, HALF], F32, name="tzg_others", tag="diff1", align_bytes=64)
        tzg = {(0, 0): first[:], (0, 1): others[:, 0, :], (1, 0): others[:, 1, :], (1, 1): others[:, 2, :]}
        for h in range(2):
            hid = sb("hid%d" % h, [P, HALF, PACK], BF16)
            cut = (HALF, HALF // 2)[h]
            nc.scalar.activation(
                hid[:, :cut, :].rearrange("p (c i) t -> p c t i", i=4),
                diff[h][:, :, :cut].rearrange("p t (c i) -> p c t i", i=4),
                ACT.Abs,
            )
            if h == 1:
                rest = diff[h][:, :, cut:].rearrange("p t c -> p c t")
                nc.vector.scalar_tensor_tensor(hid[:, cut:, :], rest, -1.0, rest, ALU.mult, ALU.max)
            hq_w = sb("hq_w%d" % h, [P, HALF], U32)
            hq_s = sb("hq_s%d" % h, [P, HALF], U8)
            nc.vector.quantize_mx(hq_w[:].bitcast(E4M3), hq_s[:], hid[:].rearrange("p c t -> p (c t)"))
            for n in range(2):
                nc.tensor.matmul_mx(
                    po[h, n][:], lhsT=wb_w[:, 2 * P * n : 2 * P * (n + 1)].bitcast(E2M1), lhsT_scale=wb_s[:, P * n : P * (n + 1)],
                    rhs=hq_w[:].bitcast(E4M3), rhs_scale=hq_s[:], start=False, stop=True,
                )
        for h in range(2):
            cols = slice(HALF * h, HALF * (h + 1))
            for n in range(2):
                gather_f32(False, tzg[h, n], tz_sb[n][:], l6[:, 8 * h : 8 * (h + 1)])
            res = sb("res%d" % h, [P, 2, HALF], F32)
            for n in range(2):
                nc.vector.tensor_tensor(res[:, n, :], po[h, n][:], tzg[h, n], ALU.add)
                if h == 1:
                    (nc.sync, nc.scalar)[n].dma_start(out[P * n : P * (n + 1), cols], res[:, n, :])
            if h == 0:
                nc.sync.dma_start(out.rearrange("(n p) o -> p n o", p=P)[:, :, cols], res[:])
